import numpy as np
CORES = [2,10,18,26,34,42,50,58,66,74,82,90,98,106,114,122]
N = 16
PERM = [[0,1],[1,2],[2,3],[3,4],[4,5],[5,6],[6,7],[7,8],[8,9],[9,10],[10,11],[11,12],[12,13],[13,14],[14,15],[15,0]]
def setup_inputs(rng):
    return {"x": rng.standard_normal((N, 128, 16), dtype=np.float32)}
def reference(x):
    y = np.empty_like(x)
    for s, d in PERM:
        y[d] = x[s]
    return {"y": y}

SCRATCH = {
    "out": ("dram", [128, 16], "float32"),
    "land": ("dram", [128, 16], "float32"),
}
SEMAPHORES = ["loaded", "read", "arrived", "stored"]

ENGINES = 8


def rank_program(g, core, T, topo):
    rank = T.rank_of(core)
    if rank is None:
        return
    perm = T.tables["PERM"]
    dsts = [d for s, d in perm if s == rank]
    n_in = len([1 for s, d in perm if d == rank])

    if dsts:
        g.dma_start(T.out[:], T.x[:]).then_inc(T.sem.loaded, 16)
        g.wait_ge(T.sem.loaded, 16)
        for d in dsts:
            dst = T.cores[d]
            rid, pid, se = topo.addr(dst)
            g.remote_dma(T.land[:], T.out[:], T.sem.arrived, T.sem.read, pid, rid,
                         topo.mask(core, dst) & ((1 << ENGINES) - 1))
    if n_in:
        g.wait_ge(T.sem.arrived, ENGINES * n_in)
        g.dma_start(T.y[:], T.land[:]).then_inc(T.sem.stored, 16)
    if dsts:
        g.wait_ge(T.sem.read, ENGINES * len(dsts))
    if n_in:
        g.wait_ge(T.sem.stored, 16)
